import numpy as np
import ml_dtypes


def mxq(x, axis, fmt="e4m3"):
    dtype, down = {"e4m3": (ml_dtypes.float8_e4m3fn, 7), "e5m2": (ml_dtypes.float8_e5m2, 14)}[fmt]
    v = np.moveaxis(np.asarray(x, np.float32).astype(ml_dtypes.bfloat16).astype(np.float64), axis, -1)
    blocks = v.reshape(v.shape[:-1] + (-1, 32))
    amax = np.abs(blocks).max(-1, keepdims=True)
    byte = np.maximum(np.where(amax > 0, np.frexp(amax)[1] - 1 + 127, 0) - down, 1)
    scale = np.exp2(byte - 127.0)
    codes = (blocks / scale).astype(np.float32).astype(dtype).astype(np.float64)
    return np.moveaxis((codes * scale).reshape(v.shape), -1, axis)


WIDE = False


def mx_kscale(k):
    if not WIDE:
        return np.ones(k)
    levels = np.array([10, -10, 5, -5, 0])
    if k % 512:
        return np.exp2(np.random.permutation(np.resize(levels, k // 32))).repeat(32)
    a = np.empty((k // 512, 16))
    for p in range(k // 512):
        a[p, :8] = np.random.permutation(np.resize(levels, 8))
        for g in range(8):
            far = levels[np.abs(levels - a[p, g]) >= 10]
            a[p, g + 8] = far[np.random.randint(len(far))]
    return np.exp2(a.ravel()).repeat(32)


BF16 = ml_dtypes.bfloat16


def bf(x):
    return np.asarray(x, np.float32).astype(BF16)


def f64(x):
    return np.asarray(x).astype(np.float64)

def planes(Y):
    n, m = Y.shape
    b = f64(bf(Y)).reshape(n // 32, 32, m)
    amax = np.abs(b).max(1)
    byte = np.clip(np.where(amax > 0, np.frexp(amax)[1] - 1 + 127 - 7, 1), 1, 254)
    codes = (b * np.exp2(127.0 - byte)[:, None, :]).reshape(n, m).astype(np.float32).astype(ml_dtypes.float8_e4m3fn).view(np.uint8)
    words = codes.reshape(n // 512, 128, 4, m).transpose(0, 1, 3, 2)
    return np.ascontiguousarray(words), np.ascontiguousarray(byte.astype(np.uint8).reshape(n // 512, 16, m))


D, F, M = 1024, 4096, 1024

HALF = 0.5


def setup_inputs():
    s = mx_kscale(F)
    g = np.exp(0.8 * np.random.randn(D))
    u = 1.5 * np.random.randn(F, M)
    h = u / (1.0 + np.exp(-u))
    w = 1.5 * np.random.randn(D, F) / np.sqrt(F) * g[:, None]
    b = 0.4 * np.random.randn(D) * g
    x = np.random.randn(D, M) * g[:, None]
    return {"h": bf(h / s[:, None]), "w": bf(w * s[None, :]), "b": bf(b), "x": bf(x)}


def reference(h, w, b, x):
    wq = mxq(f64(w), 1, "e4m3")
    hq = mxq(f64(h), 0, "e4m3")
    z = wq @ hq
    y = f64(x) + HALF * (z + f64(b)[:, None])
    Y = y
    words, scales = planes(Y)
    return y, words, scales

@@ -1,0 +1,272 @@
+from contextlib import ExitStack
+
+import concourse.mybir as mybir
+from concourse.masks import make_identity
+
+D, F, M = 1024, 4096, 1024
+FLOPS = 2 * D * F * M
+
+F32 = mybir.dt.float32
+BF16 = mybir.dt.bfloat16
+U32 = mybir.dt.uint32
+I32 = mybir.dt.int32
+U8 = mybir.dt.uint8
+FP8X4 = mybir.dt.float8_e4m3fn_x4
+ALU = mybir.AluOpType
+IDENTITY = mybir.ActivationFunctionType.Identity
+
+P = 128
+PACK = 4
+GROUP = P * PACK
+PASSES = F // GROUP
+HALF = 0.5
+RAW_BUFS = 7
+GROUPED_BUFS = 3
+VECTOR_COLS = 384
+
+
+def tile_conformer_half_step_output_g2_kernel(tc, h, w, b, x, out_0, out_1, out_2):
+    nc = tc.nc
+    with ExitStack() as ctx:
+        keep = ctx.enter_context(tc.tile_pool(name="keep", bufs=1))
+        raw = ctx.enter_context(tc.tile_pool(name="raw", bufs=RAW_BUFS))
+        stage = ctx.enter_context(tc.tile_pool(name="stage", bufs=GROUPED_BUFS))
+        psum = ctx.enter_context(tc.psum_pool(name="psum", bufs=1))
+        ctx.enter_context(tc.manual_schedule())
+
+        ident = keep.tile([P, P], F32, name="ident")
+        make_identity(nc, ident[:])
+        b_sb = keep.tile([P, 2, PACK], BF16, name="b_sb")
+        half_b = keep.tile([P, 2, PACK], F32, name="half_b")
+        nc.scalar.dma_start(out=b_sb[:], in_=b.rearrange("(g p t) -> p g t", g=2, t=PACK))
+        nc.scalar.activation(out=half_b[:], in_=b_sb[:], func=IDENTITY, scale=HALF)
+
+        w_raw, h_raw, x_sb, turned, w_grouped, h_grouped = {}, {}, {}, {}, {}, {}
+        w_codes, w_scales, h_codes, h_scales = {}, {}, {}, {}
+        acc, y_sb, y_grouped = {}, {}, {}
+        y_codes, y_scales = {}, {}
+        for g in range(2):
+            y_codes[g] = keep.tile([P, M], U32, name="y_codes%d" % g, align_bytes=64)
+            y_scales[g] = keep.tile([P, M], U8, name="y_scales%d" % g, align_bytes=64)
+
+        pieces = [(0, 0, 512, 0), (1, 0, 512, 0), (0, 512, 512, 4), (1, 512, 256, 0), (1, 768, 256, 4)]
+
+        def load_w(i):
+            g, c = divmod(i, PASSES)
+            w_raw[i] = raw.tile([P, PACK, GROUP], BF16, name="w_raw")
+            src = w[g * GROUP : (g + 1) * GROUP, c * GROUP : (c + 1) * GROUP]
+            nc.sync.dma_start(out=w_raw[i][:], in_=src.rearrange("(p t) k -> p t k", t=PACK))
+
+        def load_h(i):
+            hf, c = divmod(i, PASSES)
+            h_raw[i] = raw.tile([P, PACK, 512], BF16, name="h_raw")
+            src = h[c * GROUP : (c + 1) * GROUP, hf * 512 : (hf + 1) * 512]
+            nc.sync.dma_start(out=h_raw[i][:], in_=src.rearrange("(p j) m -> p j m", j=PACK))
+
+        def load_x(i):
+            hf, g = divmod(i, 2)
+            x_sb[g, hf] = keep.tile([P, PACK, 512], BF16, name="x%d" % i)
+            src = x[g * GROUP : (g + 1) * GROUP, hf * 512 : (hf + 1) * 512]
+            nc.sync.dma_start(out=x_sb[g, hf][:], in_=src.rearrange("(p t) m -> p t m", t=PACK))
+
+        def transpose_w(i):
+            words = w_raw[i][:].bitcast(F32)
+            for k in range(2):
+                turned[i, k] = psum.tile([P, 2, 2, P], F32, name="bank%d" % (4 + 2 * (i % 2) + k))
+                for a in range(2):
+                    for u in range(2):
+                        nc.tensor.transpose(turned[i, k][:, a, u, :], words[:, 2 * k + a, u : GROUP // 2 : 2], ident[:])
+
+        def copy_w(i):
+            w_grouped[i] = stage.tile([P, GROUP * PACK], BF16, name="w_grouped", align_bytes=64)
+            words = w_grouped[i][:].bitcast(F32)
+            for k in range(2):
+                nc.scalar.copy(
+                    out=words[:, k * 512 : (k + 1) * 512].rearrange("p (a r u) -> p a r u", a=2, u=2),
+                    in_=turned[i, k][:].rearrange("p a u r -> p a r u"),
+                )
+
+        def quantize_w(i):
+            w_codes[i] = keep.tile([P, GROUP], U32, name="w_codes%d" % i, align_bytes=64)
+            w_scales[i] = keep.tile([P, GROUP], U8, name="w_scales%d" % i, align_bytes=64)
+            nc.vector.quantize_mx(out=w_codes[i][:].bitcast(FP8X4), scales=w_scales[i][:], in_=w_grouped[i][:])
+
+        def interleave_views(dst, src, c0, c1):
+            return (
+                dst[:, c0:c1, :].rearrange("p (c i) t -> p c t i", i=4),
+                src[:, :, c0:c1].rearrange("p t (c i) -> p c t i", i=4),
+            )
+
+        def interleave_h_vector(i):
+            h_grouped[i] = stage.tile([P, 512, PACK], BF16, name="h_grouped", align_bytes=64)
+            dst, src = interleave_views(h_grouped[i], h_raw[i], 0, VECTOR_COLS)
+            nc.vector.tensor_copy(out=dst, in_=src)
+
+        def interleave_h_scalar(i):
+            dst, src = interleave_views(h_grouped[i], h_raw[i], VECTOR_COLS, 512)
+            nc.scalar.copy(out=dst, in_=src)
+
+        def quantize_h(i):
+            h_codes[i] = keep.tile([P, 512], U32, name="h_codes%d" % i, align_bytes=64)
+            h_scales[i] = keep.tile([P, 512], U8, name="h_scales%d" % i, align_bytes=64)
+            nc.vector.quantize_mx(
+                out=h_codes[i][:].bitcast(FP8X4),
+                scales=h_scales[i][:],
+                in_=h_grouped[i][:].rearrange("p m j -> p (m j)"),
+            )
+
+        def multiply(q, c, t):
+            g, m0, n, bank = pieces[q]
+            hf, off = divmod(m0, 512)
+            if c == 0:
+                acc[q, t] = psum.tile([P, n], F32, name="bank%d" % (bank + t))
+            wi, hi = g * PASSES + c, hf * PASSES + c
+            nc.tensor.matmul_mx(
+                out=acc[q, t][:],
+                lhsT=w_codes[wi][:, t * P : (t + 1) * P].bitcast(FP8X4),
+                lhsT_scale=w_scales[wi][:, t * P : (t + 1) * P],
+                rhs=h_codes[hi][:, off : off + n].bitcast(FP8X4),
+                rhs_scale=h_scales[hi][:, off : off + n],
+                start=(c == 0),
+                stop=(c == PASSES - 1),
+            )
+
+        def y_tile(q):
+            if q not in y_sb:
+                y_sb[q] = keep.tile([P, PACK, pieces[q][2]], F32, name="y%d" % q)
+            return y_sb[q]
+
+        def x_rows(q, t):
+            g, m0, n, bank = pieces[q]
+            hf, off = divmod(m0, 512)
+            return x_sb[g, hf][:, t, off : off + n]
+
+        def empty_bank(q, t, on_scalar):
+            bias = half_b[:, pieces[q][0], t : t + 1]
+            if on_scalar:
+                nc.scalar.activation(out=y_tile(q)[:, t, :], in_=acc[q, t][:], func=IDENTITY, bias=bias, scale=HALF)
+            else:
+                nc.vector.tensor_scalar(
+                    out=y_tile(q)[:, t, :], in0=acc[q, t][:], scalar1=HALF, scalar2=bias, op0=ALU.mult, op1=ALU.add
+                )
+
+        def add_x(q, t):
+            nc.vector.tensor_tensor(out=y_sb[q][:, t, :], in0=y_sb[q][:, t, :], in1=x_rows(q, t), op=ALU.add)
+
+        def start_y(q, t):
+            bias = half_b[:, pieces[q][0], t : t + 1]
+            nc.scalar.activation(out=y_tile(q)[:, t, :], in_=x_rows(q, t), func=IDENTITY, bias=bias, scale=1.0)
+
+        def finish_y(q, t):
+            nc.vector.scalar_tensor_tensor(
+                out=y_sb[q][:, t, :], in0=acc[q, t][:], scalar=HALF, in1=y_sb[q][:, t, :], op0=ALU.mult, op1=ALU.add
+            )
+
+        def interleave_y(q, on_scalar):
+            n = pieces[q][2]
+            y_grouped[q] = stage.tile([P, n, PACK], BF16, name="y_grouped", bufs=2, align_bytes=64)
+            dst, src = interleave_views(y_grouped[q], y_sb[q], 0, n)
+            if on_scalar:
+                nc.scalar.copy(out=dst, in_=src)
+            else:
+                nc.vector.tensor_copy(out=dst, in_=src)
+
+        def quantize_y(q):
+            g, m0, n, bank = pieces[q]
+            nc.vector.quantize_mx(
+                out=y_codes[g][:, m0 : m0 + n].bitcast(FP8X4),
+                scales=y_scales[g][:, m0 : m0 + n],
+                in_=y_grouped[q][:].rearrange("p m t -> p (m t)"),
+            )
+
+        def store_y(q, t0, t1):
+            g, m0, n, bank = pieces[q]
+            dst = out_0[g * GROUP : (g + 1) * GROUP, m0 : m0 + n].rearrange("(p t) m -> p t m", t=PACK)
+            nc.sync.dma_start(out=dst[:, t0:t1, :], in_=y_sb[q][:, t0:t1, :])
+
+        def store_codes(q):
+            g, m0, n, bank = pieces[q]
+            dst = out_1[g].rearrange("p m t -> p (m t)").bitcast(I32)
+            nc.sync.dma_start(out=dst[:, m0 : m0 + n], in_=y_codes[g][:, m0 : m0 + n].bitcast(I32))
+
+        def store_scales(g, engines):
+            for quad in range(4):
+                engines[quad].dma_start(
+                    out=out_2[g, 4 * quad : 4 * quad + 4, :].bitcast(I32),
+                    in_=y_scales[g][32 * quad : 32 * quad + 4, :].bitcast(I32),
+                )
+
+        chunks = 2 * PASSES
+        for i in range(RAW_BUFS):
+            load_w(i)
+            load_h(i)
+
+        steps = [([0], [])] + [([s], [s - 1]) for s in range(1, 9)]
+        steps += [([s, s + 1], [s - 1, s]) for s in range(9, 15, 2)] + [([15], [14, 15])]
+        for prepared, multiplied in steps:
+            for i in prepared:
+                transpose_w(i)
+            for i in prepared:
+                interleave_h_vector(i)
+                copy_w(i)
+                interleave_h_scalar(i)
+                quantize_w(i)
+                quantize_h(i)
+                if i + RAW_BUFS < chunks:
+                    load_w(i + RAW_BUFS)
+                    load_h(i + RAW_BUFS)
+                if i + RAW_BUFS == chunks - 1:
+                    for j in range(4):
+                        load_x(j)
+            for i in multiplied:
+                q, c = divmod(i, PASSES)
+                for t in range(PACK):
+                    multiply(q, c, t)
+                if c == PASSES - 1:
+                    for t in range(PACK):
+                        empty_bank(q, t, q == 1 or t % 2 == 0)
+
+        for c in range(PASSES):
+            for t in range(PACK):
+                multiply(2, c, t)
+        for q in (0, 1):
+            for t in range(PACK):
+                add_x(q, t)
+            store_y(q, 0, PACK)
+            interleave_y(q, True)
+        for q in (3, 4):
+            for t in range(PACK):
+                start_y(q, t)
+        for q in (0, 1):
+            quantize_y(q)
+            store_codes(q)
+        for t in range(PACK):
+            empty_bank(2, t, t % 2 == 0)
+        for t in range(PACK):
+            for c in range(PASSES):
+                multiply(3, c, t)
+            add_x(2, t)
+            finish_y(3, t)
+        store_y(2, 0, PACK)
+        interleave_y(2, True)
+        store_y(3, 0, PACK)
+        for t in range(PACK):
+            for c in range(PASSES):
+                multiply(4, c, t)
+            if t == 0:
+                interleave_y(3, False)
+            if t == 1:
+                quantize_y(3)
+                store_codes(3)
+            if t == 2:
+                quantize_y(2)
+                store_codes(2)
+                store_scales(0, [nc.sync] * 4)
+            finish_y(4, t)
+            if t == 2:
+                store_y(4, 0, 3)
+        store_y(4, 3, 4)
+        interleave_y(4, False)
+        quantize_y(4)
+        store_codes(4)
+        store_scales(1, [nc.scalar, nc.scalar, nc.sync, nc.sync])

@@ -22,7 +22,7 @@ PASSES = F // GROUP
 HALF = 0.5
 RAW_BUFS = 7
 GROUPED_BUFS = 3
-VECTOR_COLS = 384
+VECTOR_COLS = 352
 
 
 def tile_conformer_half_step_output_g2_kernel(tc, h, w, b, x, out_0, out_1, out_2):
@@ -52,10 +52,12 @@ def tile_conformer_half_step_output_g2_kernel(tc, h, w, b, x, out_0, out_1, out_
         pieces = [(0, 0, 512, 0), (1, 0, 512, 0), (0, 512, 512, 4), (1, 512, 256, 0), (1, 768, 256, 4)]
 
         def load_w(i):
-            g, c = divmod(i, PASSES)
-            w_raw[i] = raw.tile([P, PACK, GROUP], BF16, name="w_raw")
-            src = w[g * GROUP : (g + 1) * GROUP, c * GROUP : (c + 1) * GROUP]
-            nc.sync.dma_start(out=w_raw[i][:], in_=src.rearrange("(p t) k -> p t k", t=PACK))
+            g, j = divmod(i, PASSES)
+            cp, tp = divmod(j, 2)
+            w_raw[i] = raw.tile([P, 2, 2 * GROUP], BF16, name="w_raw")
+            src = w[g * GROUP : (g + 1) * GROUP, cp * 2 * GROUP : (cp + 1) * 2 * GROUP]
+            src = src.rearrange("(p t) k -> p t k", t=PACK)
+            nc.sync.dma_start(out=w_raw[i][:], in_=src[:, 2 * tp : 2 * tp + 2, :])
 
         def load_h(i):
             hf, c = divmod(i, PASSES)
@@ -63,11 +65,10 @@ def tile_conformer_half_step_output_g2_kernel(tc, h, w, b, x, out_0, out_1, out_
             src = h[c * GROUP : (c + 1) * GROUP, hf * 512 : (hf + 1) * 512]
             nc.sync.dma_start(out=h_raw[i][:], in_=src.rearrange("(p j) m -> p j m", j=PACK))
 
-        def load_x(i):
-            hf, g = divmod(i, 2)
-            x_sb[g, hf] = keep.tile([P, PACK, 512], BF16, name="x%d" % i)
-            src = x[g * GROUP : (g + 1) * GROUP, hf * 512 : (hf + 1) * 512]
-            nc.sync.dma_start(out=x_sb[g, hf][:], in_=src.rearrange("(p t) m -> p t m", t=PACK))
+        def load_x(g):
+            x_sb[g] = keep.tile([P, PACK, M], BF16, name="x%d" % g)
+            src = x[g * GROUP : (g + 1) * GROUP, :]
+            nc.sync.dma_start(out=x_sb[g][:], in_=src.rearrange("(p t) m -> p t m", t=PACK))
 
         def transpose_w(i):
             words = w_raw[i][:].bitcast(F32)
@@ -75,7 +76,7 @@ def tile_conformer_half_step_output_g2_kernel(tc, h, w, b, x, out_0, out_1, out_
                 turned[i, k] = psum.tile([P, 2, 2, P], F32, name="bank%d" % (4 + 2 * (i % 2) + k))
                 for a in range(2):
                     for u in range(2):
-                        nc.tensor.transpose(turned[i, k][:, a, u, :], words[:, 2 * k + a, u : GROUP // 2 : 2], ident[:])
+                        nc.tensor.transpose(turned[i, k][:, a, u, :], words[:, a, 256 * k + u : 256 * (k + 1) : 2], ident[:])
 
         def copy_w(i):
             w_grouped[i] = stage.tile([P, GROUP * PACK], BF16, name="w_grouped", align_bytes=64)
@@ -120,11 +121,12 @@ def tile_conformer_half_step_output_g2_kernel(tc, h, w, b, x, out_0, out_1, out_
             hf, off = divmod(m0, 512)
             if c == 0:
                 acc[q, t] = psum.tile([P, n], F32, name="bank%d" % (bank + t))
-            wi, hi = g * PASSES + c, hf * PASSES + c
+            wi, hi = g * PASSES + 2 * (c // 2) + t // 2, hf * PASSES + c
+            col = (2 * (c % 2) + t % 2) * P
             nc.tensor.matmul_mx(
                 out=acc[q, t][:],
-                lhsT=w_codes[wi][:, t * P : (t + 1) * P].bitcast(FP8X4),
-                lhsT_scale=w_scales[wi][:, t * P : (t + 1) * P],
+                lhsT=w_codes[wi][:, col : col + P].bitcast(FP8X4),
+                lhsT_scale=w_scales[wi][:, col : col + P],
                 rhs=h_codes[hi][:, off : off + n].bitcast(FP8X4),
                 rhs_scale=h_scales[hi][:, off : off + n],
                 start=(c == 0),
@@ -138,8 +140,7 @@ def tile_conformer_half_step_output_g2_kernel(tc, h, w, b, x, out_0, out_1, out_
 
         def x_rows(q, t):
             g, m0, n, bank = pieces[q]
-            hf, off = divmod(m0, 512)
-            return x_sb[g, hf][:, t, off : off + n]
+            return x_sb[g][:, t, m0 : m0 + n]
 
         def empty_bank(q, t, on_scalar):
             bias = half_b[:, pieces[q][0], t : t + 1]
@@ -201,45 +202,60 @@ def tile_conformer_half_step_output_g2_kernel(tc, h, w, b, x, out_0, out_1, out_
             load_w(i)
             load_h(i)
 
-        steps = [([0], [])] + [([s], [s - 1]) for s in range(1, 9)]
-        steps += [([s, s + 1], [s - 1, s]) for s in range(9, 15, 2)] + [([15], [14, 15])]
-        for prepared, multiplied in steps:
-            for i in prepared:
-                transpose_w(i)
-            for i in prepared:
-                interleave_h_vector(i)
-                copy_w(i)
-                interleave_h_scalar(i)
-                quantize_w(i)
-                quantize_h(i)
-                if i + RAW_BUFS < chunks:
-                    load_w(i + RAW_BUFS)
-                    load_h(i + RAW_BUFS)
-                if i + RAW_BUFS == chunks - 1:
-                    for j in range(4):
-                        load_x(j)
-            for i in multiplied:
-                q, c = divmod(i, PASSES)
+        lead = 2
+        for s in range(3 * PASSES + lead):
+            hi = s if s < PASSES else s - 1
+            has_h = hi < chunks and s != PASSES
+            if s < chunks:
+                transpose_w(s)
+            if has_h:
+                interleave_h_vector(hi)
+                interleave_h_scalar(hi)
+            if s < chunks:
+                copy_w(s)
+            if 1 <= s <= chunks:
+                quantize_w(s - 1)
+            if has_h:
+                quantize_h(hi)
+            if s + RAW_BUFS < chunks:
+                load_w(s + RAW_BUFS)
+            if has_h and hi + RAW_BUFS < chunks:
+                load_h(hi + RAW_BUFS)
+                if hi + RAW_BUFS == chunks - 1:
+                    load_x(0)
+                    load_x(1)
+            if 16 <= s < 20:
+                add_x(0, s - 16)
+            if s == 19:
+                store_y(0, 0, PACK)
+            if s in (19, 20):
+                add_x(1, 2 * (s - 19))
+                add_x(1, 2 * (s - 19) + 1)
+            if s == 20:
+                interleave_y(0, True)
+                store_y(1, 0, PACK)
+            if s == 21:
+                interleave_y(1, True)
+            if s in (22, 24):
+                quantize_y((s - 22) // 2)
+                store_codes((s - 22) // 2)
+            if s in (23, 24):
                 for t in range(PACK):
-                    multiply(q, c, t)
-                if c == PASSES - 1:
-                    for t in range(PACK):
+                    start_y(s - 20, t)
+            i = s - lead
+            if 0 <= i < chunks:
+                q, j = divmod(i, PASSES)
+                cp, tp = divmod(j, 2)
+                for c in (2 * cp, 2 * cp + 1):
+                    for t in (2 * tp, 2 * tp + 1):
+                        multiply(q, c, t)
+                if j >= PASSES - 2:
+                    for t in (2 * tp, 2 * tp + 1):
                         empty_bank(q, t, q == 1 or t % 2 == 0)
+            if i >= chunks:
+                for t in range(PACK):
+                    multiply(2, i - chunks, t)
 
-        for c in range(PASSES):
-            for t in range(PACK):
-                multiply(2, c, t)
-        for q in (0, 1):
-            for t in range(PACK):
-                add_x(q, t)
-            store_y(q, 0, PACK)
-            interleave_y(q, True)
-        for q in (3, 4):
-            for t in range(PACK):
-                start_y(q, t)
-        for q in (0, 1):
-            quantize_y(q)
-            store_codes(q)
         for t in range(PACK):
             empty_bank(2, t, t % 2 == 0)
         for t in range(PACK):

@@ -20,9 +20,11 @@ PACK = 4
 GROUP = P * PACK
 PASSES = F // GROUP
 HALF = 0.5
-RAW_BUFS = 7
+RAW_BUFS = 6
 GROUPED_BUFS = 3
-VECTOR_COLS = 352
+VECTOR_COLS = [352] * 8 + [448] * 3 + [256] * 5
+FIRST_SORTED = 10
+LOAD_ORDER = "wh" * 8 + "wwwwwhwwhwhhhxhhhx"
 
 
 def tile_conformer_half_step_output_g2_kernel(tc, h, w, b, x, out_0, out_1, out_2):
@@ -43,7 +45,9 @@ def tile_conformer_half_step_output_g2_kernel(tc, h, w, b, x, out_0, out_1, out_
 
         w_raw, h_raw, x_sb, turned, w_grouped, h_grouped = {}, {}, {}, {}, {}, {}
         w_codes, w_scales, h_codes, h_scales = {}, {}, {}, {}
-        acc, y_sb, y_grouped = {}, {}, {}
+        acc, y_sb, y_grouped, w_sorted = {}, {}, {}, {}
+        released = set()
+        pending = [(kind, sum(1 for c in LOAD_ORDER[:n] if c == kind)) for n, kind in enumerate(LOAD_ORDER)]
         y_codes, y_scales = {}, {}
         for g in range(2):
             y_codes[g] = keep.tile([P, M], U32, name="y_codes%d" % g, align_bytes=64)
@@ -70,13 +74,35 @@ def tile_conformer_half_step_output_g2_kernel(tc, h, w, b, x, out_0, out_1, out_
             src = x[g * GROUP : (g + 1) * GROUP, :]
             nc.sync.dma_start(out=x_sb[g][:], in_=src.rearrange("(p t) m -> p t m", t=PACK))
 
+        def issue_loads():
+            while pending:
+                kind, i = pending[0]
+                if kind != "x" and i >= RAW_BUFS and (kind, i - RAW_BUFS) not in released:
+                    return
+                pending.remove((kind, i))
+                loaders[kind](i)
+
+        def sort_w(i):
+            w_sorted[i] = stage.tile([P, 4, 2, P], F32, name="w_sorted")
+            words = w_raw[i][:].rearrange("p a k -> p (a k)").bitcast(F32)
+            nc.vector.tensor_copy(out=w_sorted[i][:], in_=words.rearrange("p (g r u) -> p g u r", g=4, u=2))
+            released.add(("w", i))
+            issue_loads()
+
         def transpose_w(i):
             words = w_raw[i][:].bitcast(F32)
             for k in range(2):
                 turned[i, k] = psum.tile([P, 2, 2, P], F32, name="bank%d" % (4 + 2 * (i % 2) + k))
                 for a in range(2):
                     for u in range(2):
-                        nc.tensor.transpose(turned[i, k][:, a, u, :], words[:, a, 256 * k + u : 256 * (k + 1) : 2], ident[:])
+                        if i < FIRST_SORTED:
+                            src = words[:, a, 256 * k + u : 256 * (k + 1) : 2]
+                        else:
+                            src = w_sorted[i][:, 2 * a + k, u, :]
+                        nc.tensor.transpose(turned[i, k][:, a, u, :], src, ident[:])
+            if i < FIRST_SORTED:
+                released.add(("w", i))
+                issue_loads()
 
         def copy_w(i):
             w_grouped[i] = stage.tile([P, GROUP * PACK], BF16, name="w_grouped", align_bytes=64)
@@ -100,12 +126,14 @@ def tile_conformer_half_step_output_g2_kernel(tc, h, w, b, x, out_0, out_1, out_
 
         def interleave_h_vector(i):
             h_grouped[i] = stage.tile([P, 512, PACK], BF16, name="h_grouped", align_bytes=64)
-            dst, src = interleave_views(h_grouped[i], h_raw[i], 0, VECTOR_COLS)
+            dst, src = interleave_views(h_grouped[i], h_raw[i], 0, VECTOR_COLS[i])
             nc.vector.tensor_copy(out=dst, in_=src)
 
         def interleave_h_scalar(i):
-            dst, src = interleave_views(h_grouped[i], h_raw[i], VECTOR_COLS, 512)
+            dst, src = interleave_views(h_grouped[i], h_raw[i], VECTOR_COLS[i], 512)
             nc.scalar.copy(out=dst, in_=src)
+            released.add(("h", i))
+            issue_loads()
 
         def quantize_h(i):
             h_codes[i] = keep.tile([P, 512], U32, name="h_codes%d" % i, align_bytes=64)
@@ -142,17 +170,13 @@ def tile_conformer_half_step_output_g2_kernel(tc, h, w, b, x, out_0, out_1, out_
             g, m0, n, bank = pieces[q]
             return x_sb[g][:, t, m0 : m0 + n]
 
-        def empty_bank(q, t, on_scalar):
+        def empty_bank(q, t):
             bias = half_b[:, pieces[q][0], t : t + 1]
-            if on_scalar:
-                nc.scalar.activation(out=y_tile(q)[:, t, :], in_=acc[q, t][:], func=IDENTITY, bias=bias, scale=HALF)
-            else:
-                nc.vector.tensor_scalar(
-                    out=y_tile(q)[:, t, :], in0=acc[q, t][:], scalar1=HALF, scalar2=bias, op0=ALU.mult, op1=ALU.add
-                )
+            nc.scalar.activation(out=y_tile(q)[:, t, :], in_=acc[q, t][:], func=IDENTITY, bias=bias, scale=HALF)
 
-        def add_x(q, t):
-            nc.vector.tensor_tensor(out=y_sb[q][:, t, :], in0=y_sb[q][:, t, :], in1=x_rows(q, t), op=ALU.add)
+        def add_x(q):
+            g, m0, n, bank = pieces[q]
+            nc.vector.tensor_tensor(out=y_sb[q][:], in0=y_sb[q][:], in1=x_sb[g][:, :, m0 : m0 + n], op=ALU.add)
 
         def start_y(q, t):
             bias = half_b[:, pieces[q][0], t : t + 1]
@@ -197,92 +221,121 @@ def tile_conformer_half_step_output_g2_kernel(tc, h, w, b, x, out_0, out_1, out_
                     in_=y_scales[g][32 * quad : 32 * quad + 4, :].bitcast(I32),
                 )
 
-        chunks = 2 * PASSES
-        for i in range(RAW_BUFS):
-            load_w(i)
-            load_h(i)
+        def interleave_h(i):
+            interleave_h_vector(i)
+            interleave_h_scalar(i)
 
-        lead = 2
-        for s in range(3 * PASSES + lead):
-            hi = s if s < PASSES else s - 1
-            has_h = hi < chunks and s != PASSES
-            if s < chunks:
-                transpose_w(s)
-            if has_h:
-                interleave_h_vector(hi)
-                interleave_h_scalar(hi)
-            if s < chunks:
-                copy_w(s)
-            if 1 <= s <= chunks:
+        def multiply_chunk(i):
+            q, j = divmod(i, PASSES)
+            cp, tp = divmod(j, 2)
+            for c in (2 * cp, 2 * cp + 1):
+                for t in (2 * tp, 2 * tp + 1):
+                    multiply(q, c, t)
+
+        def multiply_slot(q, t):
+            for c in range(PASSES):
+                multiply(q, c, t)
+
+        def finish_planes(q):
+            quantize_y(q)
+            store_codes(q)
+
+        loaders = {"w": load_w, "h": load_h, "x": load_x}
+        issue_loads()
+
+        for s in range(PASSES):
+            transpose_w(s)
+            interleave_h(s)
+            copy_w(s)
+            if s >= 1:
                 quantize_w(s - 1)
-            if has_h:
-                quantize_h(hi)
-            if s + RAW_BUFS < chunks:
-                load_w(s + RAW_BUFS)
-            if has_h and hi + RAW_BUFS < chunks:
-                load_h(hi + RAW_BUFS)
-                if hi + RAW_BUFS == chunks - 1:
-                    load_x(0)
-                    load_x(1)
-            if 16 <= s < 20:
-                add_x(0, s - 16)
-            if s == 19:
-                store_y(0, 0, PACK)
-            if s in (19, 20):
-                add_x(1, 2 * (s - 19))
-                add_x(1, 2 * (s - 19) + 1)
-            if s == 20:
-                interleave_y(0, True)
-                store_y(1, 0, PACK)
-            if s == 21:
-                interleave_y(1, True)
-            if s in (22, 24):
-                quantize_y((s - 22) // 2)
-                store_codes((s - 22) // 2)
-            if s in (23, 24):
-                for t in range(PACK):
-                    start_y(s - 20, t)
-            i = s - lead
-            if 0 <= i < chunks:
-                q, j = divmod(i, PASSES)
-                cp, tp = divmod(j, 2)
-                for c in (2 * cp, 2 * cp + 1):
-                    for t in (2 * tp, 2 * tp + 1):
-                        multiply(q, c, t)
-                if j >= PASSES - 2:
-                    for t in (2 * tp, 2 * tp + 1):
-                        empty_bank(q, t, q == 1 or t % 2 == 0)
-            if i >= chunks:
-                for t in range(PACK):
-                    multiply(2, i - chunks, t)
+            quantize_h(s)
+            if s >= 2:
+                multiply_chunk(s - 2)
 
+        transpose_w(8)
+        copy_w(8)
+        quantize_w(7)
+        sort_w(10)
+        multiply_chunk(6)
+        transpose_w(9)
+        empty_bank(0, 0)
+        copy_w(9)
+        empty_bank(0, 1)
+        quantize_w(8)
+        sort_w(11)
+        multiply_chunk(7)
+        empty_bank(0, 2)
+        empty_bank(0, 3)
+        quantize_w(9)
+
+        for a in (10, 12, 14):
+            hi = a // 2 + 3
+            transpose_w(a)
+            transpose_w(a + 1)
+            if a < 14:
+                sort_w(a + 2)
+            copy_w(a)
+            interleave_h(hi)
+            if a < 14:
+                sort_w(a + 3)
+            copy_w(a + 1)
+            quantize_w(a)
+            quantize_h(hi)
+            quantize_w(a + 1)
+            multiply_chunk(a - 2)
+            multiply_chunk(a - 1)
+        multiply_chunk(14)
+        multiply_chunk(15)
+
+        interleave_h(11)
+        for hi in range(12, 16):
+            interleave_h(hi)
+            quantize_h(hi - 1)
+            if hi == 13:
+                add_x(0)
+                store_y(0, 0, PACK)
+        quantize_h(15)
         for t in range(PACK):
-            empty_bank(2, t, t % 2 == 0)
+            empty_bank(1, t)
+        interleave_y(0, True)
+        add_x(1)
+        store_y(1, 0, PACK)
+        for q in (2, 3):
+            for t in range(PACK):
+                start_y(q, t)
+        finish_planes(0)
+        interleave_y(1, True)
+        for c in range(PASSES):
+            for t in range(PACK):
+                multiply(2, c, t)
         for t in range(PACK):
-            for c in range(PASSES):
-                multiply(3, c, t)
-            add_x(2, t)
-            finish_y(3, t)
+            start_y(4, t)
+
+        multiply_slot(3, 0)
+        for t in range(PACK):
+            finish_y(2, t)
         store_y(2, 0, PACK)
-        interleave_y(2, True)
-        store_y(3, 0, PACK)
-        for t in range(PACK):
-            for c in range(PASSES):
-                multiply(4, c, t)
-            if t == 0:
-                interleave_y(3, False)
+        interleave_y(2, False)
+        finish_y(3, 0)
+        for t in range(1, PACK):
+            multiply_slot(3, t)
+            finish_y(3, t)
             if t == 1:
-                quantize_y(3)
-                store_codes(3)
-            if t == 2:
-                quantize_y(2)
-                store_codes(2)
+                finish_planes(1)
+        store_y(3, 0, PACK)
+        interleave_y(3, True)
+        for t in range(PACK):
+            multiply_slot(4, t)
+            if t == 0:
+                finish_planes(2)
                 store_scales(0, [nc.sync] * 4)
             finish_y(4, t)
+            if t == 1:
+                finish_planes(3)
             if t == 2:
                 store_y(4, 0, 3)
         store_y(4, 3, 4)
         interleave_y(4, False)
-        quantize_y(4)
-        store_codes(4)
+        finish_planes(4)
         store_scales(1, [nc.scalar, nc.scalar, nc.sync, nc.sync])

@@ -22,9 +22,10 @@ PASSES = F // GROUP
 HALF = 0.5
 RAW_BUFS = 6
 GROUPED_BUFS = 3
-VECTOR_COLS = [352] * 8 + [448] * 3 + [256] * 5
-FIRST_SORTED = 10
-LOAD_ORDER = "wh" * 8 + "wwwwwhwwhwhhhxhhhx"
+VECTOR_COLS = [352] * 8 + [256] * 8
+FIRST_SORTED = 9
+WARM_PASSES = (14, 10, 10)
+LOAD_ORDER = "wh" * 8 + "wwwwwwhwwhhxhhhhhx"
 
 
 def tile_conformer_half_step_output_g2_kernel(tc, h, w, b, x, out_0, out_1, out_2):
@@ -174,9 +175,32 @@ def tile_conformer_half_step_output_g2_kernel(tc, h, w, b, x, out_0, out_1, out_
             bias = half_b[:, pieces[q][0], t : t + 1]
             nc.scalar.activation(out=y_tile(q)[:, t, :], in_=acc[q, t][:], func=IDENTITY, bias=bias, scale=HALF)
 
-        def add_x(q):
+        def add_x(q, t0, t1):
             g, m0, n, bank = pieces[q]
-            nc.vector.tensor_tensor(out=y_sb[q][:], in0=y_sb[q][:], in1=x_sb[g][:, :, m0 : m0 + n], op=ALU.add)
+            rows = y_sb[q][:, t0:t1, :]
+            nc.vector.tensor_tensor(out=rows, in0=rows, in1=x_sb[g][:, t0:t1, m0 : m0 + n], op=ALU.add)
+
+        def empty_bank_vector(q, t):
+            bias = half_b[:, pieces[q][0], t : t + 1]
+            nc.vector.tensor_scalar(
+                out=y_tile(q)[:, t, :], in0=acc[q, t][:], scalar1=HALF, scalar2=bias, op0=ALU.mult, op1=ALU.add
+            )
+
+        def warm_up(count):
+            scratch = {}
+            for j in range(count):
+                bank, part = divmod(j, 4)
+                if part == 0:
+                    scratch[bank] = psum.tile([P, 4, P], F32, name="bank%d" % bank)
+                nc.tensor.matmul_mx(
+                    out=scratch[bank][:, part, :],
+                    lhsT=warm_codes[:].bitcast(FP8X4),
+                    lhsT_scale=warm_scales[:],
+                    rhs=warm_codes[:].bitcast(FP8X4),
+                    rhs_scale=warm_scales[:],
+                    start=True,
+                    stop=True,
+                )
 
         def start_y(q, t):
             bias = half_b[:, pieces[q][0], t : t + 1]
@@ -243,7 +267,15 @@ def tile_conformer_half_step_output_g2_kernel(tc, h, w, b, x, out_0, out_1, out_
         loaders = {"w": load_w, "h": load_h, "x": load_x}
         issue_loads()
 
+        zeros = keep.tile([P, P * PACK], BF16, name="zeros", align_bytes=64)
+        warm_codes = keep.tile([P, P], U32, name="warm_codes", align_bytes=64)
+        warm_scales = keep.tile([P, P], U8, name="warm_scales", align_bytes=64)
+        nc.vector.memset(zeros[:].bitcast(I32), 0)
+        nc.vector.quantize_mx(out=warm_codes[:].bitcast(FP8X4), scales=warm_scales[:], in_=zeros[:])
+
         for s in range(PASSES):
+            if s < len(WARM_PASSES):
+                warm_up(WARM_PASSES[s])
             transpose_w(s)
             interleave_h(s)
             copy_w(s)
@@ -255,18 +287,19 @@ def tile_conformer_half_step_output_g2_kernel(tc, h, w, b, x, out_0, out_1, out_
 
         transpose_w(8)
         copy_w(8)
+        sort_w(9)
         quantize_w(7)
-        sort_w(10)
         multiply_chunk(6)
         transpose_w(9)
-        empty_bank(0, 0)
-        copy_w(9)
-        empty_bank(0, 1)
         quantize_w(8)
+        sort_w(10)
+        empty_bank(0, 0)
+        empty_bank(0, 1)
+        copy_w(9)
         sort_w(11)
         multiply_chunk(7)
         empty_bank(0, 2)
-        empty_bank(0, 3)
+        empty_bank_vector(0, 3)
         quantize_w(9)
 
         for a in (10, 12, 14):
@@ -275,37 +308,38 @@ def tile_conformer_half_step_output_g2_kernel(tc, h, w, b, x, out_0, out_1, out_
             transpose_w(a + 1)
             if a < 14:
                 sort_w(a + 2)
-            copy_w(a)
-            interleave_h(hi)
-            if a < 14:
                 sort_w(a + 3)
+            copy_w(a)
             copy_w(a + 1)
-            quantize_w(a)
-            quantize_h(hi)
-            quantize_w(a + 1)
+            if a > 10:
+                quantize_h(hi - 1)
+            interleave_h(hi)
+            for j in range(2):
+                quantize_w(a + j)
+                if a == 14:
+                    add_x(0, j, j + 1)
             multiply_chunk(a - 2)
             multiply_chunk(a - 1)
         multiply_chunk(14)
         multiply_chunk(15)
 
-        interleave_h(11)
-        for hi in range(12, 16):
+        for hi in range(11, 16):
             interleave_h(hi)
             quantize_h(hi - 1)
             if hi == 13:
-                add_x(0)
+                add_x(0, 2, PACK)
                 store_y(0, 0, PACK)
         quantize_h(15)
         for t in range(PACK):
             empty_bank(1, t)
         interleave_y(0, True)
-        add_x(1)
+        add_x(1, 0, PACK)
         store_y(1, 0, PACK)
         for q in (2, 3):
             for t in range(PACK):
                 start_y(q, t)
         finish_planes(0)
-        interleave_y(1, True)
+        interleave_y(1, False)
         for c in range(PASSES):
             for t in range(PACK):
                 multiply(2, c, t)
@@ -316,23 +350,23 @@ def tile_conformer_half_step_output_g2_kernel(tc, h, w, b, x, out_0, out_1, out_
         for t in range(PACK):
             finish_y(2, t)
         store_y(2, 0, PACK)
-        interleave_y(2, False)
+        interleave_y(2, True)
         finish_y(3, 0)
         for t in range(1, PACK):
             multiply_slot(3, t)
-            finish_y(3, t)
-            if t == 1:
+            if t == 2:
                 finish_planes(1)
+            finish_y(3, t)
         store_y(3, 0, PACK)
-        interleave_y(3, True)
+        interleave_y(3, False)
         for t in range(PACK):
             multiply_slot(4, t)
+            if t == 2:
+                finish_planes(3)
+            finish_y(4, t)
             if t == 0:
                 finish_planes(2)
                 store_scales(0, [nc.sync] * 4)
-            finish_y(4, t)
-            if t == 1:
-                finish_planes(3)
             if t == 2:
                 store_y(4, 0, 3)
         store_y(4, 3, 4)

from contextlib import ExitStack

import concourse.mybir as mybir
from concourse.masks import make_identity

D, F, M = 1024, 4096, 1024
FLOPS = 2 * D * F * M

F32 = mybir.dt.float32
BF16 = mybir.dt.bfloat16
U32 = mybir.dt.uint32
I32 = mybir.dt.int32
U8 = mybir.dt.uint8
FP8X4 = mybir.dt.float8_e4m3fn_x4
ALU = mybir.AluOpType
IDENTITY = mybir.ActivationFunctionType.Identity

P = 128
PACK = 4
GROUP = P * PACK
PASSES = F // GROUP
HALF = 0.5
RAW_BUFS = 6
GROUPED_BUFS = 3
VECTOR_COLS = [352] * 8 + [256] * 8
FIRST_SORTED = 9
WARM_PASSES = (14, 10, 10)
LOAD_ORDER = "wh" * 8 + "wwwwwwhwwhhxhhhhhx"


def tile_conformer_half_step_output_g2_kernel(tc, h, w, b, x, out_0, out_1, out_2):
    nc = tc.nc
    with ExitStack() as ctx:
        keep = ctx.enter_context(tc.tile_pool(name="keep", bufs=1))
        raw = ctx.enter_context(tc.tile_pool(name="raw", bufs=RAW_BUFS))
        stage = ctx.enter_context(tc.tile_pool(name="stage", bufs=GROUPED_BUFS))
        psum = ctx.enter_context(tc.psum_pool(name="psum", bufs=1))
        ctx.enter_context(tc.manual_schedule())

        ident = keep.tile([P, P], F32, name="ident")
        make_identity(nc, ident[:])
        b_sb = keep.tile([P, 2, PACK], BF16, name="b_sb")
        half_b = keep.tile([P, 2, PACK], F32, name="half_b")
        nc.scalar.dma_start(out=b_sb[:], in_=b.rearrange("(g p t) -> p g t", g=2, t=PACK))
        nc.scalar.activation(out=half_b[:], in_=b_sb[:], func=IDENTITY, scale=HALF)

        w_raw, h_raw, x_sb, turned, w_grouped, h_grouped = {}, {}, {}, {}, {}, {}
        w_codes, w_scales, h_codes, h_scales = {}, {}, {}, {}
        acc, y_sb, y_grouped, w_sorted = {}, {}, {}, {}
        released = set()
        pending = [(kind, sum(1 for c in LOAD_ORDER[:n] if c == kind)) for n, kind in enumerate(LOAD_ORDER)]
        y_codes, y_scales = {}, {}
        for g in range(2):
            y_codes[g] = keep.tile([P, M], U32, name="y_codes%d" % g, align_bytes=64)
            y_scales[g] = keep.tile([P, M], U8, name="y_scales%d" % g, align_bytes=64)

        pieces = [(0, 0, 512, 0), (1, 0, 512, 0), (0, 512, 512, 4), (1, 512, 256, 0), (1, 768, 256, 4)]

        def load_w(i):
            g, j = divmod(i, PASSES)
            cp, tp = divmod(j, 2)
            w_raw[i] = raw.tile([P, 2, 2 * GROUP], BF16, name="w_raw")
            src = w[g * GROUP : (g + 1) * GROUP, cp * 2 * GROUP : (cp + 1) * 2 * GROUP]
            src = src.rearrange("(p t) k -> p t k", t=PACK)
            nc.sync.dma_start(out=w_raw[i][:], in_=src[:, 2 * tp : 2 * tp + 2, :])

        def load_h(i):
            hf, c = divmod(i, PASSES)
            h_raw[i] = raw.tile([P, PACK, 512], BF16, name="h_raw")
            src = h[c * GROUP : (c + 1) * GROUP, hf * 512 : (hf + 1) * 512]
            nc.sync.dma_start(out=h_raw[i][:], in_=src.rearrange("(p j) m -> p j m", j=PACK))

        def load_x(g):
            x_sb[g] = keep.tile([P, PACK, M], BF16, name="x%d" % g)
            src = x[g * GROUP : (g + 1) * GROUP, :]
            nc.sync.dma_start(out=x_sb[g][:], in_=src.rearrange("(p t) m -> p t m", t=PACK))

        def issue_loads():
            while pending:
                kind, i = pending[0]
                if kind != "x" and i >= RAW_BUFS and (kind, i - RAW_BUFS) not in released:
                    return
                pending.remove((kind, i))
                loaders[kind](i)

        def sort_w(i):
            w_sorted[i] = stage.tile([P, 4, 2, P], F32, name="w_sorted")
            words = w_raw[i][:].rearrange("p a k -> p (a k)").bitcast(F32)
            nc.vector.tensor_copy(out=w_sorted[i][:], in_=words.rearrange("p (g r u) -> p g u r", g=4, u=2))
            released.add(("w", i))
            issue_loads()

        def transpose_w(i):
            words = w_raw[i][:].bitcast(F32)
            for k in range(2):
                turned[i, k] = psum.tile([P, 2, 2, P], F32, name="bank%d" % (4 + 2 * (i % 2) + k))
                for a in range(2):
                    for u in range(2):
                        if i < FIRST_SORTED:
                            src = words[:, a, 256 * k + u : 256 * (k + 1) : 2]
                        else:
                            src = w_sorted[i][:, 2 * a + k, u, :]
                        nc.tensor.transpose(turned[i, k][:, a, u, :], src, ident[:])
            if i < FIRST_SORTED:
                released.add(("w", i))
                issue_loads()

        def copy_w(i):
            w_grouped[i] = stage.tile([P, GROUP * PACK], BF16, name="w_grouped", align_bytes=64)
            words = w_grouped[i][:].bitcast(F32)
            for k in range(2):
                nc.scalar.copy(
                    out=words[:, k * 512 : (k + 1) * 512].rearrange("p (a r u) -> p a r u", a=2, u=2),
                    in_=turned[i, k][:].rearrange("p a u r -> p a r u"),
                )

        def quantize_w(i):
            w_codes[i] = keep.tile([P, GROUP], U32, name="w_codes%d" % i, align_bytes=64)
            w_scales[i] = keep.tile([P, GROUP], U8, name="w_scales%d" % i, align_bytes=64)
            nc.vector.quantize_mx(out=w_codes[i][:].bitcast(FP8X4), scales=w_scales[i][:], in_=w_grouped[i][:])

        def interleave_views(dst, src, c0, c1):
            return (
                dst[:, c0:c1, :].rearrange("p (c i) t -> p c t i", i=4),
                src[:, :, c0:c1].rearrange("p t (c i) -> p c t i", i=4),
            )

        def interleave_h_vector(i):
            h_grouped[i] = stage.tile([P, 512, PACK], BF16, name="h_grouped", align_bytes=64)
            dst, src = interleave_views(h_grouped[i], h_raw[i], 0, VECTOR_COLS[i])
            nc.vector.tensor_copy(out=dst, in_=src)

        def interleave_h_scalar(i):
            dst, src = interleave_views(h_grouped[i], h_raw[i], VECTOR_COLS[i], 512)
            nc.scalar.copy(out=dst, in_=src)
            released.add(("h", i))
            issue_loads()

        def quantize_h(i):
            h_codes[i] = keep.tile([P, 512], U32, name="h_codes%d" % i, align_bytes=64)
            h_scales[i] = keep.tile([P, 512], U8, name="h_scales%d" % i, align_bytes=64)
            nc.vector.quantize_mx(
                out=h_codes[i][:].bitcast(FP8X4),
                scales=h_scales[i][:],
                in_=h_grouped[i][:].rearrange("p m j -> p (m j)"),
            )

        def multiply(q, c, t):
            g, m0, n, bank = pieces[q]
            hf, off = divmod(m0, 512)
            if c == 0:
                acc[q, t] = psum.tile([P, n], F32, name="bank%d" % (bank + t))
            wi, hi = g * PASSES + 2 * (c // 2) + t // 2, hf * PASSES + c
            col = (2 * (c % 2) + t % 2) * P
            nc.tensor.matmul_mx(
                out=acc[q, t][:],
                lhsT=w_codes[wi][:, col : col + P].bitcast(FP8X4),
                lhsT_scale=w_scales[wi][:, col : col + P],
                rhs=h_codes[hi][:, off : off + n].bitcast(FP8X4),
                rhs_scale=h_scales[hi][:, off : off + n],
                start=(c == 0),
                stop=(c == PASSES - 1),
            )

        def y_tile(q):
            if q not in y_sb:
                y_sb[q] = keep.tile([P, PACK, pieces[q][2]], F32, name="y%d" % q)
            return y_sb[q]

        def x_rows(q, t):
            g, m0, n, bank = pieces[q]
            return x_sb[g][:, t, m0 : m0 + n]

        def empty_bank(q, t):
            bias = half_b[:, pieces[q][0], t : t + 1]
            nc.scalar.activation(out=y_tile(q)[:, t, :], in_=acc[q, t][:], func=IDENTITY, bias=bias, scale=HALF)

        def add_x(q, t0, t1):
            g, m0, n, bank = pieces[q]
            rows = y_sb[q][:, t0:t1, :]
            nc.vector.tensor_tensor(out=rows, in0=rows, in1=x_sb[g][:, t0:t1, m0 : m0 + n], op=ALU.add)

        def empty_bank_vector(q, t):
            bias = half_b[:, pieces[q][0], t : t + 1]
            nc.vector.tensor_scalar(
                out=y_tile(q)[:, t, :], in0=acc[q, t][:], scalar1=HALF, scalar2=bias, op0=ALU.mult, op1=ALU.add
            )

        def warm_up(count):
            scratch = {}
            for j in range(count):
                bank, part = divmod(j, 4)
                if part == 0:
                    scratch[bank] = psum.tile([P, 4, P], F32, name="bank%d" % bank)
                nc.tensor.matmul_mx(
                    out=scratch[bank][:, part, :],
                    lhsT=warm_codes[:].bitcast(FP8X4),
                    lhsT_scale=warm_scales[:],
                    rhs=warm_codes[:].bitcast(FP8X4),
                    rhs_scale=warm_scales[:],
                    start=True,
                    stop=True,
                )

        def start_y(q, t):
            bias = half_b[:, pieces[q][0], t : t + 1]
            nc.scalar.activation(out=y_tile(q)[:, t, :], in_=x_rows(q, t), func=IDENTITY, bias=bias, scale=1.0)

        def finish_y(q, t):
            nc.vector.scalar_tensor_tensor(
                out=y_sb[q][:, t, :], in0=acc[q, t][:], scalar=HALF, in1=y_sb[q][:, t, :], op0=ALU.mult, op1=ALU.add
            )

        def interleave_y(q, on_scalar):
            n = pieces[q][2]
            y_grouped[q] = stage.tile([P, n, PACK], BF16, name="y_grouped", bufs=2, align_bytes=64)
            dst, src = interleave_views(y_grouped[q], y_sb[q], 0, n)
            if on_scalar:
                nc.scalar.copy(out=dst, in_=src)
            else:
                nc.vector.tensor_copy(out=dst, in_=src)

        def quantize_y(q):
            g, m0, n, bank = pieces[q]
            nc.vector.quantize_mx(
                out=y_codes[g][:, m0 : m0 + n].bitcast(FP8X4),
                scales=y_scales[g][:, m0 : m0 + n],
                in_=y_grouped[q][:].rearrange("p m t -> p (m t)"),
            )

        def store_y(q, t0, t1):
            g, m0, n, bank = pieces[q]
            dst = out_0[g * GROUP : (g + 1) * GROUP, m0 : m0 + n].rearrange("(p t) m -> p t m", t=PACK)
            nc.sync.dma_start(out=dst[:, t0:t1, :], in_=y_sb[q][:, t0:t1, :])

        def store_codes(q):
            g, m0, n, bank = pieces[q]
            dst = out_1[g].rearrange("p m t -> p (m t)").bitcast(I32)
            nc.sync.dma_start(out=dst[:, m0 : m0 + n], in_=y_codes[g][:, m0 : m0 + n].bitcast(I32))

        def store_scales(g, engines):
            for quad in range(4):
                engines[quad].dma_start(
                    out=out_2[g, 4 * quad : 4 * quad + 4, :].bitcast(I32),
                    in_=y_scales[g][32 * quad : 32 * quad + 4, :].bitcast(I32),
                )

        def interleave_h(i):
            interleave_h_vector(i)
            interleave_h_scalar(i)

        def multiply_chunk(i):
            q, j = divmod(i, PASSES)
            cp, tp = divmod(j, 2)
            for c in (2 * cp, 2 * cp + 1):
                for t in (2 * tp, 2 * tp + 1):
                    multiply(q, c, t)

        def multiply_slot(q, t):
            for c in range(PASSES):
                multiply(q, c, t)

        def finish_planes(q):
            quantize_y(q)
            store_codes(q)

        loaders = {"w": load_w, "h": load_h, "x": load_x}
        issue_loads()

        zeros = keep.tile([P, P * PACK], BF16, name="zeros", align_bytes=64)
        warm_codes = keep.tile([P, P], U32, name="warm_codes", align_bytes=64)
        warm_scales = keep.tile([P, P], U8, name="warm_scales", align_bytes=64)
        nc.vector.memset(zeros[:].bitcast(I32), 0)
        nc.vector.quantize_mx(out=warm_codes[:].bitcast(FP8X4), scales=warm_scales[:], in_=zeros[:])

        for s in range(PASSES):
            if s < len(WARM_PASSES):
                warm_up(WARM_PASSES[s])
            transpose_w(s)
            interleave_h(s)
            copy_w(s)
            if s >= 1:
                quantize_w(s - 1)
            quantize_h(s)
            if s >= 2:
                multiply_chunk(s - 2)

        transpose_w(8)
        copy_w(8)
        sort_w(9)
        quantize_w(7)
        multiply_chunk(6)
        transpose_w(9)
        quantize_w(8)
        sort_w(10)
        empty_bank(0, 0)
        empty_bank(0, 1)
        copy_w(9)
        sort_w(11)
        multiply_chunk(7)
        empty_bank(0, 2)
        empty_bank_vector(0, 3)
        quantize_w(9)

        for a in (10, 12, 14):
            hi = a // 2 + 3
            transpose_w(a)
            transpose_w(a + 1)
            if a < 14:
                sort_w(a + 2)
                sort_w(a + 3)
            copy_w(a)
            copy_w(a + 1)
            if a > 10:
                quantize_h(hi - 1)
            interleave_h(hi)
            for j in range(2):
                quantize_w(a + j)
                if a == 14:
                    add_x(0, j, j + 1)
            multiply_chunk(a - 2)
            multiply_chunk(a - 1)
        multiply_chunk(14)
        multiply_chunk(15)

        for hi in range(11, 16):
            interleave_h(hi)
            quantize_h(hi - 1)
            if hi == 13:
                add_x(0, 2, PACK)
                store_y(0, 0, PACK)
        quantize_h(15)
        for t in range(PACK):
            empty_bank(1, t)
        interleave_y(0, True)
        add_x(1, 0, PACK)
        store_y(1, 0, PACK)
        for q in (2, 3):
            for t in range(PACK):
                start_y(q, t)
        finish_planes(0)
        interleave_y(1, False)
        for c in range(PASSES):
            for t in range(PACK):
                multiply(2, c, t)
        for t in range(PACK):
            start_y(4, t)

        multiply_slot(3, 0)
        for t in range(PACK):
            finish_y(2, t)
        store_y(2, 0, PACK)
        interleave_y(2, True)
        finish_y(3, 0)
        for t in range(1, PACK):
            multiply_slot(3, t)
            if t == 2:
                finish_planes(1)
            finish_y(3, t)
        store_y(3, 0, PACK)
        interleave_y(3, False)
        for t in range(PACK):
            multiply_slot(4, t)
            if t == 2:
                finish_planes(3)
            finish_y(4, t)
            if t == 0:
                finish_planes(2)
                store_scales(0, [nc.sync] * 4)
            if t == 2:
                store_y(4, 0, 3)
        store_y(4, 3, 4)
        interleave_y(4, False)
        finish_planes(4)
        store_scales(1, [nc.scalar, nc.scalar, nc.sync, nc.sync])
